import numpy as np, ml_dtypes
CORES = [3,11,19,27,35,43,51,59]
N = 8
import mx_ref
BF = ml_dtypes.bfloat16
def gcols(t, e):
    v = np.concatenate([t.reshape(8, 16, -1, 4), np.zeros((8, 16, 1, 4), BF)], axis=2)
    return np.ascontiguousarray(np.stack([v[g][:, e[g]] for g in range(8)])).reshape(128, -1)
def tile(rs):
    return np.stack(rs, axis=2).reshape(128, -1).astype(BF)
def cut(t, i, w=512):
    return t[:, w * i:w * i + w]
def pick(q, e):
    c = np.concatenate([q[0].reshape(128, -1, 4), np.zeros((128, 1, 4), np.uint8)], axis=1); s = np.concatenate([q[1], np.ones((16, 1), np.uint8)], axis=1)
    return (np.ascontiguousarray(c[:, e].reshape(128, -1)), np.ascontiguousarray(s[:, e]))
def join(*qs):
    return (np.concatenate([q[0] for q in qs], axis=1), np.concatenate([q[1] for q in qs], axis=1))
def put(q, e, v):
    c, s = q[0].reshape(128, -1, 4).copy(), q[1].copy(); c[:, e] = v[0].reshape(128, -1, 4); s[:, e] = v[1]
    return (c.reshape(128, -1), s)
def pk(c, s):
    return (np.ascontiguousarray(c), mx_ref.live(s))
def emit(q):
    return q[0], q[1]
def packed(v, rng):
    q = [mx_ref.quantize(np.ascontiguousarray(v[r])) for r in range(N)]
    return np.stack([a for a, b in q]), np.stack([mx_ref.plane(b, rng) for a, b in q])
def values_of_codes():
    e, c = np.zeros((128, 128, 4), np.float32), np.zeros((128, 2, 4), np.uint8)
    e[np.arange(128), np.arange(128), 0] = 1
    c[:127, :, 0] = np.arange(256).reshape(2, 128).T[:127]
    return mx_ref.matmul(mx_ref.quantize(e.reshape(128, 512).astype(BF)), (c.reshape(128, 8), np.full((16, 2), 127, np.uint8))).T.reshape(-1).astype(np.float64)
CODE_VALUE, SCALE_VALUE = values_of_codes(), 2.0 ** (np.arange(256) - 127.0)
def decode(q):
    return (CODE_VALUE[q[0]].reshape(16, 8, -1, 4) * SCALE_VALUE[q[1]][:, None, :, None] + 0.0).reshape(128, -1).astype(np.float32)
def f(rng, *shape):
    return mx_ref.flush((rng.standard_normal(shape, dtype=np.float32) * np.exp2(rng.integers(-2, 3, shape[:-1] + (1,)))).astype(BF))
def wide(rng, *shape, cols=0):
    v = rng.standard_normal(shape, dtype=np.float32) * np.exp2(rng.integers(-12, 13, shape)).astype(np.float32)
    if cols: v *= np.repeat(np.exp2(rng.integers(-cols, cols + 1, shape[:-2] + (1, shape[-1] // 4))) * (rng.random(shape[:-2] + (1, shape[-1] // 4)) > 0.0625), 4, axis=-1).astype(np.float32)
    return mx_ref.flush(v.astype(BF))
C, A, R = 384, 128, 3
STEP = [1, 2, 4]
def parse(b, a):
    word = 64 * b[:, :-3] + 16 * b[:, 1:-2] + 4 * b[:, 2:-1] + b[:, 3:]
    block = 64 * a[:, ::4] + 16 * a[:, 1::4] + 4 * a[:, 2::4] + a[:, 3::4]
    first = np.full((8, 256), -1)
    for m in range(C // 4 - 1, -1, -1): first[np.arange(8), block[:, m]] = m
    found = np.concatenate([np.take_along_axis(first, word, axis=1), np.full((8, 3), -1)], axis=1)
    h = np.zeros((8, C), np.int64)
    go, shift, lits = np.zeros(8, np.int64), np.zeros(8, np.int64), np.zeros(8, np.int64)
    for c in range(C):
        run = (go == c) & (found[:, c] >= 0)
        lit = (go == c) & (found[:, c] < 0)
        shift = np.where(run, 4 * found[:, c] - c, shift)
        h[:, c] = np.where(lit, np.where(lits < A, C + c, c), c + shift)
        lits = lits + lit
        go = np.where(run, c + 4, np.where(lit, c + 1, go))
    return h
def numbers_of(rng):
    return {"x": np.array(f(rng, N, 128, 4 * C)), "u": np.array(f(rng, N, 128, 512)), "v": np.array(f(rng, N, 128, 512))}
def weights(rng, still=[]):
    w = np.array(f(rng, N, 128, 2048)).reshape(N, 8, 16, 4, 8, 16, 4)
    for i in still:
        w[:, :, i] = 0
        w[:, :, :, :, :, i] = 0
    c, p = packed(w.reshape(N, 128, 2048), rng)
    return {"wc": c, "ws": p}
def signs(rng):
    return np.stack([rng.permutation(8) % 2 * 2.0 - 1.0 for r in range(N)])
def planted(rng, z, size, k):
    d = numbers_of(rng)
    x = d["x"].astype(np.float32).reshape(N, 8, 16, C, 4)
    x[:, :, :8] = 0
    for i, b in enumerate((z // 2, z % 2)): x[:, :, i, :, 0] = np.where(b > 0, 1, -rng.integers(0, 2, z.shape)) * size
    u = d["u"].reshape(N, 128, 128, 4)
    for h in range(0, 128, 16):
        u[:, :, h:h + 2] = 0
        for i in range(2): u[:, h + i, h + i, 0] = k
    return {"x": x.reshape(N, 128, 4 * C).astype(BF), "u": u.reshape(N, 128, 512), "v": d["v"], **weights(rng, range(8))}
def setup_inputs(rng):
    return {**numbers_of(rng), **weights(rng)}
def setup_inputs_ties(rng):
    per = rng.permutation([1, 2, 3, 4, 5, 8, 12, 16])
    s = rng.integers(0, 240, (N, 8))
    z = np.zeros((N, 8, C), np.int64)
    for g in range(8):
        pat = rng.integers(0, 4, per[g])
        if per[g] == 1: pat[:] = rng.integers(1, 4)
        if per[g] == 4:
            pat = rng.permutation(4)
            s[1::2, g] = s[::2, g] + rng.integers(1, 4, N // 2)
        z[:, g] = pat[(s[:, g, None] + np.arange(C)) % per[g]]
        if per[g] in (1, 3):
            other = int(rng.choice(np.setdiff1d(np.arange(4), pat)))
            for r in range(0, N, 2): z[r, g, :int(rng.integers(1, 4))] = other
    d = planted(rng, z, 1.0, np.ones(N, np.float32).astype(BF))
    d["x"][rng.integers(N)] = 0
    return d
def setup_inputs_near(rng):
    low = rng.permutation(N) < N // 2
    size = np.exp2(np.where(low[:, None, None], -30.0, rng.integers(-30, 31, (N, 8, C))))
    d = planted(rng, rng.integers(0, 4, (N, 8, C)), size, np.where(low, 2.0 ** -30, 1.0).astype(np.float32).astype(BF))
    x, u = d["x"].reshape(N, 8, 16, C, 4), d["u"].reshape(N, 128, 128, 4)
    for r in range(N):
        if low[r]:
            k = x[r, :, :2, :, 0].astype(np.float32)
            least = (k > 0) & (rng.integers(0, 2, k.shape) > 0)
            x[r, :, :2, :, 0] = np.where(least, 2.25 * 2.0 ** -30, k).astype(np.float32).astype(BF)
            x[r, :, 2:4, :, 0] = np.where(least, -1.625 * 2.0 ** -30, 0.0).astype(np.float32).astype(BF)
            for h in range(0, 128, 16):
                for i in range(2): u[r, h + 2 + i, h + i, 0] = 1.375 * 2.0 ** -30
    return {"x": x.reshape(N, 128, 4 * C), "u": u.reshape(N, 128, 512), "v": d["v"], "wc": d["wc"], "ws": d["ws"]}
def setup_inputs_caps(rng):
    words = (rng.permutation(16)[:8, None] >> np.arange(4)) & 1
    late = rng.permutation(N // 2) % 2
    z = np.zeros((N, 8, C), np.int64)
    for r in range(N):
        if r % 2 == 0: h = int(rng.integers(8))
        n = np.insert(rng.permutation([0, 4, A - 4, A, A + 4, 2 * A, C - 32]), h, C)
        own = 2 + r % 2
        for g in range(8):
            if g == h:
                z[r, g] = own
                if late[r // 2]: z[r, g, r % 2 * (C - 4) + np.arange(4)] = words[0]
                continue
            k = rng.permutation(np.concatenate([np.full(n[g], -1), rng.integers(0, 8, (C - 32 - n[g]) // 4)]))
            mixed = np.concatenate([words[i] if i >= 0 else [own] for i in k])
            blocks = words[rng.permutation(8)].reshape(-1)
            z[r, g] = np.concatenate([mixed, blocks] if rng.integers(2) else [blocks, mixed])
    return planted(rng, z, 1.0, np.ones(N, np.float32).astype(BF))
def setup_inputs_huge(rng):
    d = numbers_of(rng)
    x = 2.0 ** 30 * (0.8 + 0.2 * rng.random((N, 128, C, 4)))
    for r in range(N): x[r][:, rng.permutation(C)[:C // 4 + 1]] = 2.0 ** 30
    c = np.ones((N, C))
    half = int(rng.integers(2))
    for r in range(N):
        if 2 * r // N == half: c[r] = rng.permutation(C) % 2 * 2.0 - 1.0
    x *= c[:, None, :, None]
    u = d["u"].reshape(N, 128, 8, 16, 4)
    h = int(rng.integers(8))
    s = np.stack([signs(rng), signs(rng)], axis=2)
    s = s * s[:, h:h + 1]
    a = 2.0 ** 30 * (1 - 0.1 * rng.random((N, 128, 8, 2, 4))) * s[:, None, :, :, None]
    a[:, :, h] = 2.0 ** 30
    u[:, :, :, :2] = a.astype(np.float32).astype(BF)
    w = np.zeros((N, 128, 4, 128, 4), np.float32)
    i = np.arange(128)
    for b in range(4): w[:, i, b, i, b] = -1
    wc, ws = packed(w.reshape(N, 128, 2048).astype(BF), rng)
    return {"x": x.astype(np.float32).reshape(N, 128, 4 * C).astype(BF), "u": u.reshape(N, 128, 512), "v": d["v"], "wc": wc, "ws": ws}
def setup_inputs_spread(rng):
    d = setup_inputs(rng)
    d["x"] = wide(rng, N, 128, 4 * C, cols=6)
    return d
def check_inputs(d):
    b = []
    for k in ("x", "u", "v"):
        a = np.abs(d[k].astype(np.float32))
        if not (np.isfinite(a).all() and ((a == 0) | (a >= 2.0 ** -30) & (a <= 2.0 ** 30)).all()): b.append("a value of " + k)
    if ((d["wc"] & 0x7F) == 0x7F).any(): b.append("a code of wc that is no number")
    z = np.zeros((128, 4, 4), np.float32)
    z[:, 1] = 2.0 ** -30
    z[:, 2] = 2.0 ** 30
    c, s = emit(mx_ref.quantize(z.reshape(128, 16).astype(BF)))
    for r in range(N):
        p = mx_ref.live(d["ws"][r])
        if not ((p == s[0, 0]) | (p >= s[0, 1]) & (p <= s[0, 2])).all(): b.append("a scale of ws")
    return b
def reference(x, u, v, wc, ws):
    qu = [mx_ref.quantize(u[r]) for r in range(N)]
    lay = [pk(wc[r], ws[r]) for r in range(N)]
    now = [x[r] for r in range(N)]
    for t in range(R):
        sent, z = [], []
        for r in range(N):
            q = mx_ref.quantize(now[r])
            p = mx_ref.matmul(qu[r], q)
            sent.append(q)
            z.append(2 * (p[::16] > 0).astype(np.int64) + (p[1::16] > 0))
        came = decode(join(*sent)).astype(BF)
        made, lists = [], []
        for r in range(N):
            e = r ^ STEP[t]
            h = parse(z[e], z[r])
            c = gcols(np.concatenate([now[r], cut(came, e, 4 * C)], axis=1), h)
            q = mx_ref.quantize(c)
            made.append(tile([mx_ref.matmul(pick(lay[r], np.arange(128 * b, 128 * b + 128)), q) * np.float32(0.015625) + c[:, b::4].astype(np.float32) for b in range(4)]))
            lists.append(h)
        now = made
    y, ot = np.zeros((N, 128, C), np.float32), np.zeros((N, 8, C), np.float32)
    oc, osc = np.zeros((N, 128, 4 * C), np.uint8), np.zeros((N, 16, C), np.uint8)
    for r in range(N):
        q = mx_ref.quantize(now[r])
        y[r] = mx_ref.matmul(mx_ref.quantize(v[r]), q)
        ot[r] = lists[r]
        oc[r], osc[r] = emit(q)
    return {"y": y, "ot": ot, "oc": oc, "osc": osc}

@@ -1,0 +1,363 @@
+from concourse.mybir import dt, AluOpType, ActivationFunctionType
+
+C, ROUNDS, STEP = 384, 3, [1, 2, 4]
+F32, BF16, F16, I32, U16, Q4, U8 = "float32", "bfloat16", "float16", "int32", "uint16", "float8_e4m3fn_x4", "uint8"
+HALF = C // 2
+TAB = 640
+
+SCRATCH = {
+    "x0": ("sbuf", [128, 4 * C], BF16), "ut": ("sbuf", [128, 512], BF16), "vt": ("sbuf", [128, 512], BF16),
+    "qu": ("sbuf", [128, 128], Q4), "su": ("sbuf", [128, 128], U8),
+    "qu2": ("sbuf", [128, 256], Q4), "su2": ("sbuf", [128, 256], U8),
+    "qv": ("sbuf", [128, 128], Q4), "sv": ("sbuf", [128, 128], U8),
+    "qw": ("sbuf", [128, 512], Q4), "sw": ("sbuf", [128, 512], U8),
+    "ones": ("sbuf", [128, TAB], BF16), "eb": ("sbuf", [128, 516], BF16),
+    "qe": ("sbuf", [128, 512], Q4), "se": ("sbuf", [128, 512], U8),
+    "ip": ("sbuf", [128, 1], I32), "qi": ("sbuf", [128, 1], I32), "qf": ("sbuf", [128, 1], F32),
+    "col": ("sbuf", [128, 6], F32), "iu": ("sbuf", [128, 16], I32), "uoff": ("sbuf", [128, 16], U16),
+    "j97": ("sbuf", [128, 97], F32), "m4": ("sbuf", [128, 96], F32), "d97": ("sbuf", [128, 97], F32),
+    "e0": ("sbuf", [128, 16], F32), "e1": ("sbuf", [128, 16], F32), "pat": ("sbuf", [128, 16], F32),
+    "qoff": ("sbuf", [128, 24], U16),
+    "selw": ("sbuf", [128, C], F32), "selh": ("sbuf", [128, C], BF16), "selc": ("sbuf", [128, C], BF16),
+    "cd0": ("sbuf", [128, 2 * C], F32), "pd1": ("sbuf", [128, 2 * C], F32), "c4": ("sbuf", [128, 588], F16),
+    "bits": ("sbuf", [128, 2 * C], F32), "cod": ("sbuf", [128, 776], F32), "wsel": ("sbuf", [128, C], F32),
+    "blk": ("sbuf", [128, 98], F16), "bsel": ("sbuf", [128, 96], F32), "tgt": ("sbuf", [128, 6], F32),
+    "ne": ("sbuf", [128, 588], F16), "fin": ("sbuf", [128, 588], F16), "soff": ("sbuf", [128, 6], U16),
+    "pd0": ("sbuf", [128, 2 * C], F32), "key": ("sbuf", [128, C], BF16), "vb": ("sbuf", [128, 770], F32),
+    "xi": ("sbuf", [128, C], I32), "yi": ("sbuf", [128, C], I32), "hd0": ("sbuf", [128, C], F16),
+    "hold": ("sbuf", [128, C], F16), "hmid": ("sbuf", [128, 1], F32), "hsel": ("sbuf", [128, C], F16),
+    "sg": ("sbuf", [128, C], BF16),
+    "csel": ("sbuf", [128, C], BF16), "l0": ("sbuf", [128, 24], F32), "lw": ("sbuf", [128, 24], F32),
+    "si": ("sbuf", [128, 24], I32), "sa": ("sbuf", [128, 24], F32), "sb": ("sbuf", [128, 24], I32),
+    "sm": ("sbuf", [128, 24], F32), "ofp": ("sbuf", [128, 32], F32), "goff": ("sbuf", [128, 24], U16),
+    "ht": ("sbuf", [128, 32], F32),
+    "gt": ("sbuf", [128, 4 * C], BF16), "g64": ("sbuf", [128, 4 * C], BF16), "xt": ("sbuf", [128, 4 * C], BF16),
+    "qg": ("sbuf", [128, C], Q4), "sgq": ("sbuf", [128, C], U8), "ysb": ("sbuf", [128, C], F32),
+    "ps": ("psum", [128, 512 * 8], F32),
+}
+for _t in range(ROUNDS):
+    SCRATCH["lc%d" % _t] = ("sbuf", [128, C], Q4)
+    SCRATCH["ls%d" % _t] = ("sbuf", [128, C], U8)
+    SCRATCH["lw%d" % _t] = ("sbuf", [128, 24], U16)
+    SCRATCH["wd%d" % _t] = ("sbuf", [128, 24], U16)
+    SCRATCH["kt%d" % _t] = ("sbuf", [128, TAB], F32)
+    SCRATCH["at%d" % _t] = ("sbuf", [128, TAB], F32)
+for _t in range(ROUNDS + 1):
+    SCRATCH["win%d" % _t] = ("sbuf", [128, 8 * C], BF16)
+    SCRATCH["qx%d" % _t] = ("sbuf", [128, C], Q4)
+    SCRATCH["sx%d" % _t] = ("sbuf", [128, C], U8)
+
+POOL = 110
+SEMAPHORES = (["c%d" % i for i in range(POOL)] + ["ldx0", "ldx1", "ldu", "ldw", "lds", "ldv", "sts", "sta", "sent"]
+              + ["%s%d" % (n, t) for n in ("ac", "ad", "aw") for t in range(ROUNDS)])
+
+NONE = 512.0
+BASE = 13400032
+SHRINK = 0.75 - 2.0 ** -23
+UNIT = 62.5
+CUT = 360
+
+
+def rank_program(g, core, T, topo):
+    rank = T.rank_of(core)
+    if rank is None:
+        return
+    A, ACT = AluOpType, ActivationFunctionType
+    queue = {"v": g.vector, "a": g.scalar, "p": g.tensor, "g": g, "s": g.sync}
+    ops = []
+
+    def op(q, fn, r=(), w=(), sem=None, n=1):
+        ops.append({"q": q, "fn": fn, "r": list(r), "w": list(w), "sem": sem, "n": n})
+
+    def ts(out, in0, s1, s2, o0, o1, r, w):
+        if o1 is None:
+            op("v", lambda: g.vector.tensor_scalar(out, in0, s1, None, o0), r, w)
+        else:
+            op("v", lambda: g.vector.tensor_scalar(out, in0, s1, s2, o0, o1), r, w)
+
+    def tt(out, in0, in1, o, r, w):
+        op("v", lambda: g.vector.tensor_tensor(out, in0, in1, o), r, w)
+
+    def cp(out, in_, r, w):
+        op("v", lambda: g.vector.tensor_copy(out, in_), r, w)
+
+    def scan(out, d0, d1, init, o0, o1, r, w):
+        op("v", lambda: g.vector.tensor_tensor_scan(out, d0, d1, init, o0, o1), r, w)
+
+    def fill(ap, c, w):
+        op("v", lambda: g.vector.memset(ap, c), [], w)
+
+    def quant(q, s, t, r, w):
+        op("v", lambda: g.vector.quantize_mx(q, s, t), r, w)
+
+    def act(out, in_, r, w, func=None, **kw):
+        op("a", lambda: g.scalar.activation(out, in_, ACT.Copy if func is None else func, **kw), r, w)
+
+    def afill(ap, n, c, w):
+        act(ap, T.ones[:, 0:n], ["ones"], w, ACT.Identity, bias=c, scale=0.0)
+
+    def mm(bank, n, ql, sl, qr, sr, r):
+        op("p", lambda: g.tensor.matmul_mx(T.ps[:, 512 * bank:512 * bank + n], ql, sl, qr, sr, True, True), r, ["ps%d" % bank])
+
+    def ps(bank, n):
+        return T.ps[:, 512 * bank:512 * bank + n]
+
+    def dma(q, out, in_, r, w, sem):
+        op(q, lambda: queue[q].dma_start(out, in_), r, w, sem, 16)
+
+    def iota(out, pat, base, mult, w, small):
+        if small:
+            op("g", lambda: g.iota(out, pat, base, mult, allow_small_or_imprecise_dtypes=True), [], w)
+        else:
+            op("g", lambda: g.iota(out, pat, base, mult), [], w)
+
+    sent = [0]
+
+    def send(t, out, in_, sem, r):
+        peer = T.cores[rank ^ STEP[t]]
+        rid, pid = topo.addr(peer)[0:2]
+        sent[0] += len(topo.engines(core, peer))
+        op("g", lambda: g.remote_dma(out, in_, T.sem[sem], T.sem.sent, pid, rid, topo.mask(core, peer)), r, [], "none")
+
+    def arrival(t, sem, calls, w):
+        peer = T.cores[rank ^ STEP[t]]
+        op("x", None, [], w, sem, calls * len(topo.engines(peer, core)))
+
+    def cols(h):
+        return slice(HALF * h, HALF * h + HALF)
+
+    def xkeys(h):
+        return ["x%d%d" % (b, h) for b in range(4)]
+
+    dma("a", T.ut[:], T.u[:], [], ["ut"], "ldu")
+    for h in range(2):
+        dma("s", T.x0[:, 2 * C * h:2 * C * h + 2 * C], T.x[:, 2 * C * h:2 * C * h + 2 * C], [], xkeys(h), "ldx%d" % h)
+    dma("s", T.qw[:].bitcast(dt.uint8), T.wc[:], [], ["qw"], "ldw")
+    dma("s", T.sw[:], T.ws[:], [], ["sw"], "lds")
+    dma("s", T.vt[:], T.v[:], [], ["vt"], "ldv")
+
+    fill(T.ones[:], 1.0, ["ones"])
+    fill(T.cod[:, 2 * C:776], 628.0 / UNIT, ["codt"])
+    fill(T.vb[:, 0:1], float(BASE + 124), ["vb0"])
+    fill(T.ofp[:, 24:32], 0.0, ["ofpt"])
+    iota(T.ip[:], [[0, 1]], 0, 1, ["ip"], False)
+    iota(T.iu[:], [[1, 2], [16, 8]], 0, 0, ["iu"], False)
+    iota(T.j97[:], [[1, 97]], 0, 0, ["j97"], True)
+    iota(T.m4[:], [[4, 96]], 0, 0, ["m4"], True)
+    op("g", lambda: g.affine_select(T.eb[:], T.ones[:, 0:516], [[1, 516]], A.is_equal, 0.0, -3, -4), ["ones"], ["eb"])
+    afill(T.cd0[:, 0:2 * C:2], C, 0.05, ["cd0a"])
+    afill(T.cd0[:, 1:2 * C:2], C, 4.0, ["cd0b"])
+    ts(T.qi[:], T.ip[:], 15, None, A.bitwise_and, None, ["ip"], ["qi"])
+    cp(T.uoff[:], T.iu[:], ["iu"], ["uoff"])
+    cp(T.qf[:], T.qi[:], ["qi"], ["qf"])
+    ts(T.blk[:, 0:1], T.j97[:, 0:1], 0.0, None, A.mult, None, ["j97"], ["blk0"])
+    qf = T.qf[:, 0:1]
+    ts(T.d97[:], T.j97[:], qf, None, A.subtract, None, ["j97", "qf"], ["d97"])
+    ts(T.qoff[:], T.j97[:, 0:24], 0.0, qf, A.mult, A.add, ["j97", "qf"], ["qoff"])
+    ts(T.col[:, 0:1], qf, 15.0, 1024.0, A.is_lt, A.mult, ["qf"], ["col0"])
+    ts(T.e0[:], T.d97[:, 0:16], 0.0, -4.0, A.is_equal, A.mult, ["d97"], ["e0"])
+    ts(T.e1[:], T.d97[:, 0:16], 1.0, None, A.is_equal, None, ["d97"], ["e1"])
+    ts(T.col[:, 1:2], T.col[:, 0:1], UNIT, None, A.mult, None, ["col0"], ["col1"])
+    tt(T.pat[:], T.e0[:], T.e1[:], A.add, ["e0", "e1"], ["pat"])
+    quant(T.qu[:], T.su[:], T.ut[:], ["ut"], ["qu"])
+    ts(T.c4[:, 97:588:98], T.m4[:, 0:24:4], qf, 1024.0, A.add, A.add, ["m4", "qf"], ["c4t"])
+    cp(T.qu2[:].bitcast(dt.uint32), T.qu[:].bitcast(dt.uint32).indirect(T.uoff[:]), ["qu", "uoff"], ["qu2"])
+    act(T.su2[:], T.su[:].indirect(T.uoff[:]), ["qu", "uoff"], ["su2"])
+    act(T.selw[:], T.pat[:].indirect(T.qoff[:]), ["pat", "qoff"], ["selw"], scale=1024.0)
+    for k in range(6):
+        ts(T.c4[:, 98 * k:98 * k + 97], T.d97[:], 16.0 * k + 1, -1024.0, A.is_equal, A.mult, ["d97"], ["c4%d" % k])
+    C4 = ["c4%d" % k for k in range(6)]
+
+    def tables(t):
+        afill(T["at%d" % t][:], TAB, SHRINK, ["at%d" % t])
+        afill(T["kt%d" % t][:], TAB, NONE, ["kt%d" % t])
+
+    tables(0)
+
+    def quant_x(t, h):
+        tile = T.x0 if t == 0 else T.xt
+        quant(T["qx%d" % t][:, cols(h)], T["sx%d" % t][:, cols(h)], tile[:, 2 * C * h:2 * C * h + 2 * C], xkeys(h), ["qx%d%d" % (t, h)])
+
+    quant_x(0, 0)
+    quant_x(0, 1)
+    for t in range(ROUNDS):
+        win, nxt, qx, sx = T["win%d" % t], T["win%d" % (t + 1)], T["qx%d" % t], T["sx%d" % t]
+        lc, ls, lwd, wd, kt, at = T["lc%d" % t], T["ls%d" % t], T["lw%d" % t], T["wd%d" % t], T["kt%d" % t], T["at%d" % t]
+        QX, KT, AT, LW, WD = ["qx%d0" % t, "qx%d1" % t], "kt%d" % t, "at%d" % t, "lw%d" % t, "wd%d" % t
+        LC = ["lc%d0" % t, "lc%d1" % t]
+        send(t, lc[:, cols(0)].bitcast(dt.uint8), qx[:, cols(0)].bitcast(dt.uint8), "ac%d" % t, QX[:1])
+        send(t, ls[:], sx[:], "ac%d" % t, QX)
+        for h in range(2):
+            for s in range(2):
+                mm(2 * h + s, HALF, T.qu2[:, 128 * s:128 * s + 128], T.su2[:, 128 * s:128 * s + 128],
+                   qx[:, cols(h)], sx[:, cols(h)], [QX[h], "qu2", "su2"])
+        for h in range(2):
+            act(T.bits[:, C * h + 1:C * h + C:2], ps(2 * h + 1, HALF), [], ["ps%d" % (2 * h + 1), "bb%d" % h], ACT.Sign, bias=-2.0 ** -110)
+        ts(T.bits[:, 0:C:2], ps(0, HALF), 0.0, 0.6584, A.is_gt, A.add, [], ["ps0", "ba0"])
+        scan(T.cod[:, 0:CUT], T.cd0[:, 0:CUT], T.bits[:, 0:CUT], 2.042, A.mult, A.add, ["cd0a", "cd0b", "ba0", "bb0"], ["cod0"])
+        ts(T.bits[:, C:2 * C:2], ps(2, HALF), 0.0, 0.6584, A.is_gt, A.add, [], ["ps2", "ba1"])
+        scan(T.cod[:, CUT:2 * C], T.cd0[:, CUT:2 * C], T.bits[:, CUT:2 * C], T.cod[:, CUT - 1:CUT], A.mult, A.add,
+             ["cod0", "ba0", "bb0", "ba1", "bb1"], ["cod1"])
+        scan(T.wsel[:, 0:176], T.selw[:, 0:176], T.cod[:, 7:359:2], 0.0, A.add, A.max, ["selw", "cod0"], ["wsel0"])
+        scan(T.wsel[:, 176:C], T.selw[:, 176:C], T.cod[:, 359:775:2], 0.0, A.add, A.max, ["selw", "cod0", "cod1", "codt"], ["wsel1"])
+        ts(wd[:], T.wsel[:, 15:C:16], UNIT, T.col[:, 1:2], A.mult, A.subtract, ["wsel0", "wsel1", "col1"], [WD])
+        send(t, lwd[:], wd[:], "aw%d" % t, [WD])
+        send(t, lc[:, cols(1)].bitcast(dt.uint8), qx[:, cols(1)].bitcast(dt.uint8), "ad%d" % t, QX[1:])
+        ts(T.blk[:, 1:97], T.cod[:, 7:775:8], UNIT, 1024.0, A.mult, A.add, ["cod0", "cod1"], ["blk"])
+        if t == 0:
+            ts(T.c4[:, 0:588:98], T.j97[:, 0:6], 0.0, 2048.0, A.mult, A.add, ["j97"], C4)
+            afill(T.pd1[:, 0:2 * C:2], C, 5.0, ["pd1a"])
+            afill(T.pd1[:, 1:2 * C:2], C, -4.0, ["pd1b"])
+            act(T.selh[:], T.selw[:], ["selw"], ["selh"], scale=-2.0)
+            afill(T.pd1[:, 7:2 * C:8], C // 4, -8.0, ["pd1b"])
+            act(T.selc[:], T.selw[:], ["selw"], ["selc"], scale=1.0 / 256)
+            for b in range(4):
+                act(win[:, 2 * C * b:2 * C * b + C], T.x0[:, b:4 * C:4], xkeys(0) + xkeys(1), ["y%d0" % b, "y%d1" % b], scale=64.0)
+        else:
+            tables(t)
+        scan(T.bsel[:], T.selw[:, 0:96], T.blk[:, 1:97], 0.0, A.add, A.max, ["selw", "blk"], ["bsel"])
+        ts(T.tgt[:], T.bsel[:, 15:96:16], T.col[:, 0:1], None, A.subtract, None, ["bsel", "col0"], ["tgt"])
+        ts(T.ne[:, 97:588:98], T.bsel[:, 15:96:16], T.col[:, 0:1], 1024.0, A.subtract, A.subtract, ["bsel", "col0"], ["net"])
+        for k in range(6):
+            ts(T.ne[:, 98 * k:98 * k + 97], T.blk[:, 0:97], T.tgt[:, k:k + 1], 640.0, A.not_equal, A.mult, ["blk", "blk0", "tgt"], ["ne%d" % k])
+        scan(T.fin[:], T.c4[:], T.ne[:], 0.0, A.add, A.min, C4 + ["c4t", "net"] + ["ne%d" % k for k in range(6)], ["fin"])
+        cp(T.soff[:], T.fin[:, 97:588:98], ["fin"], ["soff"])
+        cp(at[:].indirect(T.soff[:]), T.ones[:, 0:96], ["soff", "ones"], [AT])
+        cp(kt[:].indirect(T.soff[:]), T.m4[:], ["soff", "m4"], [KT])
+        if t == 0:
+            ts(T.col[:, 2:3], T.col[:, 0:1], -0.75, qf, A.mult, A.add, ["col0", "qf"], ["col2"])
+            ts(T.col[:, 4:5], T.col[:, 0:1], -2.0, NONE, A.mult, A.add, ["col0"], ["col4"])
+            ts(T.col[:, 5:6], T.col[:, 0:1], 2.0, None, A.mult, None, ["col0"], ["col5"])
+            ts(T.col[:, 3:4], T.col[:, 2:3], 192.0, None, A.add, None, ["col2"], ["col3"])
+            for b in range(4):
+                quant(T.qe[:, 128 * b:128 * b + 128], T.se[:, 128 * b:128 * b + 128], T.eb[:, 3 - b:515 - b], ["eb"], ["qe%d" % b])
+        if t == 1:
+            quant(T.qv[:], T.sv[:], T.vt[:], ["vt"], ["qv"])
+        arrival(t, "aw%d" % t, 1, [LW])
+        arrival(t, "ac%d" % t, 2, LC[:1])
+        arrival(t, "ad%d" % t, 1, LC[1:])
+        act(T.pd0[:, 0:2 * C:2], at[:].indirect(lwd[:]), [AT, LW], ["pda"])
+        ts(T.pd0[:, 1:2 * C:2], kt[:].indirect(lwd[:]), 384.0, 1.0 / 384.0, A.max, A.mult, [KT, LW], ["pdb"])
+        act(T.key[:], kt[:].indirect(lwd[:]), [KT, LW], ["key"])
+        for h in range(2):
+            for b in range(4):
+                mm(4 * (1 - h) + b, HALF, T.qe[:, 128 * b:128 * b + 128], T.se[:, 128 * b:128 * b + 128],
+                   lc[:, cols(h)], ls[:, cols(h)], LC[:h + 1] + ["qe%d" % b])
+        scan(T.vb[:, 1:2 * C + 1], T.pd0[:], T.pd1[:], float(BASE + 124), A.mult, A.add, ["pda", "pdb", "pd1a", "pd1b"], ["vb"])
+        for k in range(8):
+            h, b = k // 4, k % 4
+            if k == 2:
+                act(T.sg[:], T.vb[:, 0:2 * C:2], ["vb", "vb0"], ["sg"], ACT.Sign, bias=float(2 - BASE))
+            lo = 2 * C * b + C + HALF * h
+            act(win[:, lo:lo + HALF], ps(4 * (1 - h) + b, HALF), [], ["ps%d" % (4 * (1 - h) + b), "d%d%d" % (b, h)], scale=64.0)
+        for h in range(2):
+            ts(T.xi[:, cols(h)], T.vb[:, C * h:C * h + C:2], float(BASE - 512), 8192.0, A.subtract, A.mult, ["vb", "vb0"], ["xi%d" % h])
+        for h in range(2):
+            ts(T.yi[:, cols(h)], T.xi[:, cols(h)], 3 << 13, None, A.bitwise_and, None, ["xi%d" % h], ["yi%d" % h])
+        for h in range(2):
+            ts(T.hd0[:, cols(h)], T.yi[:, cols(h)], 4096.0, 513.0, A.subtract, A.min, ["yi%d" % h], ["hd%d" % h])
+        scan(T.csel[:], T.selc[:], T.sg[:], 0.0, A.add, A.max, ["selc", "sg"], ["csel"])
+        scan(T.hold[:], T.hd0[:], T.key[:], 0.0, A.add, A.max, ["hd0", "hd1", "key"], ["hold"])
+        ts(T.l0[:], T.csel[:, 15:C:16], 192.0, T.col[:, 3:4], A.mult, A.add, ["csel", "col3"], ["l0"])
+        scan(T.hsel[:], T.selh[:], T.hold[:], 0.0, A.add, A.min, ["selh", "hold"], ["hsel"])
+        tt(T.lw[:], T.l0[:], T.m4[:, 0:96:4], A.add, ["l0", "m4"], ["lw"])
+        ts(T.sa[:], T.hsel[:, 15:C:16], T.col[:, 4:5], 4096.0, A.is_equal, A.mult, ["hsel", "col4"], ["sa"])
+        ts(T.si[:], T.hsel[:, 15:C:16], T.col[:, 5:6], None, A.add, None, ["hsel", "col5"], ["si"])
+        tt(T.sm[:], T.sa[:], T.lw[:], A.min, ["sa", "lw"], ["sm"])
+        ts(T.sb[:], T.si[:], 511, None, A.bitwise_and, None, ["si"], ["sb"])
+        tt(T.ofp[:, 0:24], T.sm[:], T.sb[:], A.max, ["sm", "sb"], ["ofp"])
+        cp(T.goff[:], T.ofp[:, 0:24], ["ofp"], ["goff"])
+        for b in range(4):
+            src = win[:, 2 * C * b:2 * C * b + 2 * C].indirect(T.goff[:])
+            need = ["y%d0" % b, "y%d1" % b, "d%d0" % b, "d%d1" % b, "goff"]
+            if b < 2:
+                ts(T.gt[:, b:4 * C:4], src, 0.015625, None, A.mult, None, need, ["g%d" % b])
+            else:
+                act(T.gt[:, b:4 * C:4], src, need, ["g%d" % b], scale=0.015625)
+        G = ["g%d" % b for b in range(4)]
+        for h in range(2):
+            quant(T.qg[:, cols(h)], T.sgq[:, cols(h)], T.gt[:, 2 * C * h:2 * C * h + 2 * C], G, ["qg%d" % h])
+        for h in range(2):
+            for b in range(4):
+                mm(4 * h + b, HALF, T.qw[:, 128 * b:128 * b + 128], T.sw[:, 128 * b:128 * b + 128],
+                   T.qg[:, cols(h)], T.sgq[:, cols(h)], ["qg%d" % h, "qw", "sw"])
+        ts(T.g64[:, 0:HALF], T.gt[:, 0:2 * C:4], 64.0, None, A.mult, None, ["g0"], ["h00"])
+        for b in range(1, 4):
+            act(T.g64[:, C * b:C * b + C], T.gt[:, b:4 * C:4], ["g%d" % b], ["h%d0" % b, "h%d1" % b], scale=64.0)
+        act(T.g64[:, HALF:C], T.gt[:, 2 * C:4 * C:4], ["g0"], ["h01"], scale=64.0)
+        if t == ROUNDS - 1:
+            op("v", lambda: g.vector.transpose(T.ht[:], T.ofp[:]), ["ofp", "ofpt"], ["ht"])
+            for k in range(8):
+                dma("s", T.ot[k, :], T.ht[32 * (k // 2):32 * (k // 2) + 24, 16 * (k % 2):16 * (k % 2) + 16], ["ht"], [], "sts")
+        for h in range(2):
+            for b in range(4):
+                lo = 2 * C * b + HALF * h
+                tt(nxt[:, lo:lo + HALF], ps(4 * h + b, HALF), T.g64[:, C * b + HALF * h:C * b + HALF * h + HALF], A.add,
+                   ["h%d%d" % (b, h)], ["ps%d" % (4 * h + b), "y%d%d" % (b, h)])
+        for h, b in [(0, 0), (0, 1), (0, 2), (0, 3), (1, 0), (1, 1)]:
+            lo = 2 * C * b + HALF * h
+            act(T.xt[:, 2 * C * h + b:2 * C * h + 2 * C:4], nxt[:, lo:lo + HALF], ["y%d%d" % (b, h)], ["x%d%d" % (b, h)], scale=0.015625)
+        quant_x(t + 1, 0)
+        for b in range(2, 4):
+            lo = 2 * C * b + HALF
+            ts(T.xt[:, 2 * C + b:4 * C:4], nxt[:, lo:lo + HALF], 0.015625, None, A.mult, None, ["y%d1" % b], ["x%d1" % b])
+        quant_x(t + 1, 1)
+
+    qx, sx = T.qx3, T.sx3
+    for h in range(2):
+        mm(h, HALF, T.qv[:], T.sv[:], qx[:, cols(h)], sx[:, cols(h)], ["qx3%d" % h, "qv"])
+        dma("s", T.oc[:, 2 * C * h:2 * C * h + 2 * C], qx[:, cols(h)].bitcast(dt.uint8), ["qx3%d" % h], [], "sts")
+    act(T.ysb[:, cols(0)], ps(0, HALF), [], ["ps0", "ys0"])
+    cp(T.ysb[:, cols(1)], ps(1, HALF), [], ["ps1", "ys1"])
+    dma("a", T.y[:, cols(0)], T.ysb[:, cols(0)], ["ys0"], [], "sta")
+    for k in range(4):
+        dma("a" if k % 2 else "s", T.osc[4 * k:4 * k + 4, :], sx[32 * k:32 * k + 4, :], ["qx30", "qx31"], [], "sta" if k % 2 else "sts")
+    dma("s", T.y[:, cols(1)], T.ysb[:, cols(1)], ["ys1"], [], "sts")
+
+    writer, readers, known = {}, {}, {q: 0 for q in "vapgsx"}
+    for i, o in enumerate(ops):
+        deps = set()
+        for k in o["r"] + o["w"]:
+            if k in writer:
+                deps.add(writer[k])
+        for k in o["w"]:
+            deps.update(readers.get(k, []))
+        o["waits"] = []
+        for d in sorted(deps, reverse=True):
+            if not known[o["q"]] >> d & 1:
+                o["waits"].append(d)
+                known[o["q"]] |= ops[d]["known"] | 1 << d
+                ops[d]["waited"] = True
+        o["known"] = known[o["q"]]
+        for k in o["r"]:
+            readers.setdefault(k, []).append(i)
+        for k in o["w"]:
+            writer[k] = i
+            readers[k] = []
+    last_on, count, total = [], [], {}
+    for i, o in enumerate(ops):
+        if o["sem"] is not None:
+            total[o["sem"]] = total.get(o["sem"], 0) + o["n"]
+            o["val"] = total[o["sem"]]
+        elif o.get("waited"):
+            free = [s for s in range(len(last_on)) if o["known"] >> last_on[s] & 1]
+            if free:
+                s = free[0]
+            else:
+                s = len(last_on)
+                last_on.append(i)
+                count.append(0)
+            last_on[s] = i
+            count[s] += 1
+            o["sem"], o["val"] = "c%d" % s, count[s]
+    for o in ops:
+        if o["q"] == "x":
+            continue
+        for d in o["waits"]:
+            queue[o["q"]].wait_ge(T.sem[ops[d]["sem"]], ops[d]["val"])
+        ins = o["fn"]()
+        if o["sem"] is not None and o["sem"] != "none":
+            ins.then_inc(T.sem[o["sem"]], o["n"])
+    g.sync.wait_ge(T.sem.sts, total["sts"])
+    g.scalar.wait_ge(T.sem.sta, total["sta"])
+    g.wait_ge(T.sem.sent, sent[0])

@@ -4,48 +4,20 @@ C, ROUNDS, STEP = 384, 3, [1, 2, 4]
 F32, BF16, F16, I32, U16, Q4, U8 = "float32", "bfloat16", "float16", "int32", "uint16", "float8_e4m3fn_x4", "uint8"
 HALF = C // 2
 TAB = 640
-
-SCRATCH = {
-    "x0": ("sbuf", [128, 4 * C], BF16), "ut": ("sbuf", [128, 512], BF16), "vt": ("sbuf", [128, 512], BF16),
-    "qu": ("sbuf", [128, 128], Q4), "su": ("sbuf", [128, 128], U8),
-    "qu2": ("sbuf", [128, 256], Q4), "su2": ("sbuf", [128, 256], U8),
-    "qv": ("sbuf", [128, 128], Q4), "sv": ("sbuf", [128, 128], U8),
-    "qw": ("sbuf", [128, 512], Q4), "sw": ("sbuf", [128, 512], U8),
-    "ones": ("sbuf", [128, TAB], BF16), "eb": ("sbuf", [128, 516], BF16),
-    "qe": ("sbuf", [128, 512], Q4), "se": ("sbuf", [128, 512], U8),
-    "ip": ("sbuf", [128, 1], I32), "qi": ("sbuf", [128, 1], I32), "qf": ("sbuf", [128, 1], F32),
-    "col": ("sbuf", [128, 6], F32), "iu": ("sbuf", [128, 16], I32), "uoff": ("sbuf", [128, 16], U16),
-    "j97": ("sbuf", [128, 97], F32), "m4": ("sbuf", [128, 96], F32), "d97": ("sbuf", [128, 97], F32),
-    "e0": ("sbuf", [128, 16], F32), "e1": ("sbuf", [128, 16], F32), "pat": ("sbuf", [128, 16], F32),
-    "qoff": ("sbuf", [128, 24], U16),
-    "selw": ("sbuf", [128, C], F32), "selh": ("sbuf", [128, C], BF16), "selc": ("sbuf", [128, C], BF16),
-    "cd0": ("sbuf", [128, 2 * C], F32), "pd1": ("sbuf", [128, 2 * C], F32), "c4": ("sbuf", [128, 588], F16),
-    "bits": ("sbuf", [128, 2 * C], F32), "cod": ("sbuf", [128, 776], F32), "wsel": ("sbuf", [128, C], F32),
-    "blk": ("sbuf", [128, 98], F16), "bsel": ("sbuf", [128, 96], F32), "tgt": ("sbuf", [128, 6], F32),
-    "ne": ("sbuf", [128, 588], F16), "fin": ("sbuf", [128, 588], F16), "soff": ("sbuf", [128, 6], U16),
-    "pd0": ("sbuf", [128, 2 * C], F32), "key": ("sbuf", [128, C], BF16), "vb": ("sbuf", [128, 770], F32),
-    "xi": ("sbuf", [128, C], I32), "yi": ("sbuf", [128, C], I32), "hd0": ("sbuf", [128, C], F16),
-    "hold": ("sbuf", [128, C], F16), "hmid": ("sbuf", [128, 1], F32), "hsel": ("sbuf", [128, C], F16),
-    "sg": ("sbuf", [128, C], BF16),
-    "csel": ("sbuf", [128, C], BF16), "l0": ("sbuf", [128, 24], F32), "lw": ("sbuf", [128, 24], F32),
-    "si": ("sbuf", [128, 24], I32), "sa": ("sbuf", [128, 24], F32), "sb": ("sbuf", [128, 24], I32),
-    "sm": ("sbuf", [128, 24], F32), "ofp": ("sbuf", [128, 32], F32), "goff": ("sbuf", [128, 24], U16),
-    "ht": ("sbuf", [128, 32], F32),
-    "gt": ("sbuf", [128, 4 * C], BF16), "g64": ("sbuf", [128, 4 * C], BF16), "xt": ("sbuf", [128, 4 * C], BF16),
-    "qg": ("sbuf", [128, C], Q4), "sgq": ("sbuf", [128, C], U8), "ysb": ("sbuf", [128, C], F32),
-    "ps": ("psum", [128, 512 * 8], F32),
-}
-for _t in range(ROUNDS):
-    SCRATCH["lc%d" % _t] = ("sbuf", [128, C], Q4)
-    SCRATCH["ls%d" % _t] = ("sbuf", [128, C], U8)
-    SCRATCH["lw%d" % _t] = ("sbuf", [128, 24], U16)
-    SCRATCH["wd%d" % _t] = ("sbuf", [128, 24], U16)
-    SCRATCH["kt%d" % _t] = ("sbuf", [128, TAB], F32)
-    SCRATCH["at%d" % _t] = ("sbuf", [128, TAB], F32)
-for _t in range(ROUNDS + 1):
-    SCRATCH["win%d" % _t] = ("sbuf", [128, 8 * C], BF16)
-    SCRATCH["qx%d" % _t] = ("sbuf", [128, C], Q4)
-    SCRATCH["sx%d" % _t] = ("sbuf", [128, C], U8)
+SCRATCH = {"ps": ("psum", [128, 512 * 8], F32)}
+for _d, _names in [
+        (BF16, dict(x0=4 * C, ut=512, vt=512, ones=TAB, eb=516, selh=C, selc=C, key=C, sg=C, csel=C, gt=4 * C, g64=4 * C, xt=4 * C,
+                    win0=8 * C, win1=8 * C, win2=8 * C, win3=8 * C)),
+        (Q4, dict(qu=128, qu2=256, qv=128, qw=512, qe=512, qg=C, qx0=C, qx1=C, qx2=C, qx3=C, lc0=C, lc1=C, lc2=C)),
+        (U8, dict(su=128, su2=256, sv=128, sw=512, se=512, sgq=C, sx0=C, sx1=C, sx2=C, sx3=C, ls0=C, ls1=C, ls2=C)),
+        (I32, dict(ip=1, qi=1, iu=16, xi=C, yi=C, si=24, sb=24)),
+        (U16, dict(uoff=16, qoff=24, soff=6, goff=24, lw0=24, lw1=24, lw2=24, wd0=24, wd1=24, wd2=24)),
+        (F16, dict(c4=588, blk=98, ne=588, fin=588, hd0=C, hold=C, hsel=C)),
+        (F32, dict(qf=1, col=6, j97=97, m4=96, d97=97, e0=16, e1=16, pat=16, selw=C, cd0=2 * C, pd1=2 * C, bits=2 * C, cod=776,
+                   wsel=C, bsel=96, tgt=6, pd0=2 * C, vb=770, l0=24, lw=24, sa=24, sm=24, ofp=32, ht=32, ysb=C,
+                   kt0=TAB, kt1=TAB, kt2=TAB, at0=TAB, at1=TAB, at2=TAB))]:
+    for _n in _names:
+        SCRATCH[_n] = ("sbuf", [128, _names[_n]], _d)
 
 POOL = 110
 SEMAPHORES = (["c%d" % i for i in range(POOL)] + ["ldx0", "ldx1", "ldu", "ldw", "lds", "ldv", "sts", "sta", "sent"]
@@ -132,23 +104,20 @@ def rank_program(g, core, T, topo):
     dma("a", T.ut[:], T.u[:], [], ["ut"], "ldu")
     for h in range(2):
         dma("s", T.x0[:, 2 * C * h:2 * C * h + 2 * C], T.x[:, 2 * C * h:2 * C * h + 2 * C], [], xkeys(h), "ldx%d" % h)
-    dma("s", T.qw[:].bitcast(dt.uint8), T.wc[:], [], ["qw"], "ldw")
-    dma("s", T.sw[:], T.ws[:], [], ["sw"], "lds")
-    dma("s", T.vt[:], T.v[:], [], ["vt"], "ldv")
 
     fill(T.ones[:], 1.0, ["ones"])
     fill(T.cod[:, 2 * C:776], 628.0 / UNIT, ["codt"])
     fill(T.vb[:, 0:1], float(BASE + 124), ["vb0"])
     fill(T.ofp[:, 24:32], 0.0, ["ofpt"])
     iota(T.ip[:], [[0, 1]], 0, 1, ["ip"], False)
-    iota(T.iu[:], [[1, 2], [16, 8]], 0, 0, ["iu"], False)
     iota(T.j97[:], [[1, 97]], 0, 0, ["j97"], True)
-    iota(T.m4[:], [[4, 96]], 0, 0, ["m4"], True)
+    iota(T.iu[:], [[1, 2], [16, 8]], 0, 0, ["iu"], False)
     op("g", lambda: g.affine_select(T.eb[:], T.ones[:, 0:516], [[1, 516]], A.is_equal, 0.0, -3, -4), ["ones"], ["eb"])
+    iota(T.m4[:], [[4, 96]], 0, 0, ["m4"], True)
     afill(T.cd0[:, 0:2 * C:2], C, 0.05, ["cd0a"])
     afill(T.cd0[:, 1:2 * C:2], C, 4.0, ["cd0b"])
+    afill(T.at0[:], TAB, SHRINK, ["at0"])
     ts(T.qi[:], T.ip[:], 15, None, A.bitwise_and, None, ["ip"], ["qi"])
-    cp(T.uoff[:], T.iu[:], ["iu"], ["uoff"])
     cp(T.qf[:], T.qi[:], ["qi"], ["qf"])
     ts(T.blk[:, 0:1], T.j97[:, 0:1], 0.0, None, A.mult, None, ["j97"], ["blk0"])
     qf = T.qf[:, 0:1]
@@ -157,28 +126,25 @@ def rank_program(g, core, T, topo):
     ts(T.col[:, 0:1], qf, 15.0, 1024.0, A.is_lt, A.mult, ["qf"], ["col0"])
     ts(T.e0[:], T.d97[:, 0:16], 0.0, -4.0, A.is_equal, A.mult, ["d97"], ["e0"])
     ts(T.e1[:], T.d97[:, 0:16], 1.0, None, A.is_equal, None, ["d97"], ["e1"])
-    ts(T.col[:, 1:2], T.col[:, 0:1], UNIT, None, A.mult, None, ["col0"], ["col1"])
+    cp(T.uoff[:], T.iu[:], ["iu"], ["uoff"])
     tt(T.pat[:], T.e0[:], T.e1[:], A.add, ["e0", "e1"], ["pat"])
+    act(T.selw[:], T.pat[:].indirect(T.qoff[:]), ["pat", "qoff"], ["selw"], scale=1024.0)
+    ts(T.col[:, 1:2], T.col[:, 0:1], UNIT, None, A.mult, None, ["col0"], ["col1"])
+    for k in range(6):
+        ts(T.c4[:, 98 * k + 1:98 * k + 97], T.d97[:, 1:97], 16.0 * k + 1, -1024.0, A.is_equal, A.mult, ["d97"], ["c4%d" % k])
+    ts(T.c4[:, 0:588:98], T.j97[:, 0:6], 0.0, 2048.0, A.mult, A.add, ["j97"], ["c4h"])
+    C4 = ["c4%d" % k for k in range(6)] + ["c4h", "c4t"]
     quant(T.qu[:], T.su[:], T.ut[:], ["ut"], ["qu"])
-    ts(T.c4[:, 97:588:98], T.m4[:, 0:24:4], qf, 1024.0, A.add, A.add, ["m4", "qf"], ["c4t"])
+    quant(T.qe[:, 0:128], T.se[:, 0:128], T.eb[:, 3:515], ["eb"], ["qe0"])
     cp(T.qu2[:].bitcast(dt.uint32), T.qu[:].bitcast(dt.uint32).indirect(T.uoff[:]), ["qu", "uoff"], ["qu2"])
     act(T.su2[:], T.su[:].indirect(T.uoff[:]), ["qu", "uoff"], ["su2"])
-    act(T.selw[:], T.pat[:].indirect(T.qoff[:]), ["pat", "qoff"], ["selw"], scale=1024.0)
-    for k in range(6):
-        ts(T.c4[:, 98 * k:98 * k + 97], T.d97[:], 16.0 * k + 1, -1024.0, A.is_equal, A.mult, ["d97"], ["c4%d" % k])
-    C4 = ["c4%d" % k for k in range(6)]
-
-    def tables(t):
-        afill(T["at%d" % t][:], TAB, SHRINK, ["at%d" % t])
-        afill(T["kt%d" % t][:], TAB, NONE, ["kt%d" % t])
-
-    tables(0)
 
     def quant_x(t, h):
         tile = T.x0 if t == 0 else T.xt
         quant(T["qx%d" % t][:, cols(h)], T["sx%d" % t][:, cols(h)], tile[:, 2 * C * h:2 * C * h + 2 * C], xkeys(h), ["qx%d%d" % (t, h)])
 
     quant_x(0, 0)
+    quant(T.qe[:, 128:256], T.se[:, 128:256], T.eb[:, 2:514], ["eb"], ["qe1"])
     quant_x(0, 1)
     for t in range(ROUNDS):
         win, nxt, qx, sx = T["win%d" % t], T["win%d" % (t + 1)], T["qx%d" % t], T["sx%d" % t]
@@ -186,7 +152,6 @@ def rank_program(g, core, T, topo):
         QX, KT, AT, LW, WD = ["qx%d0" % t, "qx%d1" % t], "kt%d" % t, "at%d" % t, "lw%d" % t, "wd%d" % t
         LC = ["lc%d0" % t, "lc%d1" % t]
         send(t, lc[:, cols(0)].bitcast(dt.uint8), qx[:, cols(0)].bitcast(dt.uint8), "ac%d" % t, QX[:1])
-        send(t, ls[:], sx[:], "ac%d" % t, QX)
         for h in range(2):
             for s in range(2):
                 mm(2 * h + s, HALF, T.qu2[:, 128 * s:128 * s + 128], T.su2[:, 128 * s:128 * s + 128],
@@ -196,46 +161,56 @@ def rank_program(g, core, T, topo):
         ts(T.bits[:, 0:C:2], ps(0, HALF), 0.0, 0.6584, A.is_gt, A.add, [], ["ps0", "ba0"])
         scan(T.cod[:, 0:CUT], T.cd0[:, 0:CUT], T.bits[:, 0:CUT], 2.042, A.mult, A.add, ["cd0a", "cd0b", "ba0", "bb0"], ["cod0"])
         ts(T.bits[:, C:2 * C:2], ps(2, HALF), 0.0, 0.6584, A.is_gt, A.add, [], ["ps2", "ba1"])
+        scan(T.wsel[:, 0:176], T.selw[:, 0:176], T.cod[:, 7:359:2], 0.0, A.add, A.max, ["selw", "cod0"], ["wsel0"])
         scan(T.cod[:, CUT:2 * C], T.cd0[:, CUT:2 * C], T.bits[:, CUT:2 * C], T.cod[:, CUT - 1:CUT], A.mult, A.add,
              ["cod0", "ba0", "bb0", "ba1", "bb1"], ["cod1"])
-        scan(T.wsel[:, 0:176], T.selw[:, 0:176], T.cod[:, 7:359:2], 0.0, A.add, A.max, ["selw", "cod0"], ["wsel0"])
         scan(T.wsel[:, 176:C], T.selw[:, 176:C], T.cod[:, 359:775:2], 0.0, A.add, A.max, ["selw", "cod0", "cod1", "codt"], ["wsel1"])
+        ts(T.blk[:, 1:97], T.cod[:, 7:775:8], UNIT, 1024.0, A.mult, A.add, ["cod0", "cod1"], ["blk"])
         ts(wd[:], T.wsel[:, 15:C:16], UNIT, T.col[:, 1:2], A.mult, A.subtract, ["wsel0", "wsel1", "col1"], [WD])
         send(t, lwd[:], wd[:], "aw%d" % t, [WD])
+        send(t, ls[:], sx[:], "ac%d" % t, QX)
         send(t, lc[:, cols(1)].bitcast(dt.uint8), qx[:, cols(1)].bitcast(dt.uint8), "ad%d" % t, QX[1:])
-        ts(T.blk[:, 1:97], T.cod[:, 7:775:8], UNIT, 1024.0, A.mult, A.add, ["cod0", "cod1"], ["blk"])
+        if t > 0:
+            afill(at[:], TAB, SHRINK, [AT])
+        afill(kt[:], TAB, NONE, [KT])
         if t == 0:
-            ts(T.c4[:, 0:588:98], T.j97[:, 0:6], 0.0, 2048.0, A.mult, A.add, ["j97"], C4)
             afill(T.pd1[:, 0:2 * C:2], C, 5.0, ["pd1a"])
             afill(T.pd1[:, 1:2 * C:2], C, -4.0, ["pd1b"])
             act(T.selh[:], T.selw[:], ["selw"], ["selh"], scale=-2.0)
             afill(T.pd1[:, 7:2 * C:8], C // 4, -8.0, ["pd1b"])
             act(T.selc[:], T.selw[:], ["selw"], ["selc"], scale=1.0 / 256)
-            for b in range(4):
+            for b in range(2):
                 act(win[:, 2 * C * b:2 * C * b + C], T.x0[:, b:4 * C:4], xkeys(0) + xkeys(1), ["y%d0" % b, "y%d1" % b], scale=64.0)
-        else:
-            tables(t)
         scan(T.bsel[:], T.selw[:, 0:96], T.blk[:, 1:97], 0.0, A.add, A.max, ["selw", "blk"], ["bsel"])
+        if t == 0:
+            ts(T.c4[:, 97:588:98], T.m4[:, 0:24:4], qf, 1024.0, A.add, A.add, ["m4", "qf"], ["c4t"])
         ts(T.tgt[:], T.bsel[:, 15:96:16], T.col[:, 0:1], None, A.subtract, None, ["bsel", "col0"], ["tgt"])
         ts(T.ne[:, 97:588:98], T.bsel[:, 15:96:16], T.col[:, 0:1], 1024.0, A.subtract, A.subtract, ["bsel", "col0"], ["net"])
         for k in range(6):
             ts(T.ne[:, 98 * k:98 * k + 97], T.blk[:, 0:97], T.tgt[:, k:k + 1], 640.0, A.not_equal, A.mult, ["blk", "blk0", "tgt"], ["ne%d" % k])
-        scan(T.fin[:], T.c4[:], T.ne[:], 0.0, A.add, A.min, C4 + ["c4t", "net"] + ["ne%d" % k for k in range(6)], ["fin"])
+        if t == 0:
+            ts(T.col[:, 2:3], T.col[:, 0:1], -0.75, qf, A.mult, A.add, ["col0", "qf"], ["col2"])
+        scan(T.fin[:], T.c4[:], T.ne[:], 0.0, A.add, A.min, C4 + ["net"] + ["ne%d" % k for k in range(6)], ["fin"])
+        if t == 0:
+            ts(T.col[:, 4:5], T.col[:, 0:1], -2.0, NONE, A.mult, A.add, ["col0"], ["col4"])
         cp(T.soff[:], T.fin[:, 97:588:98], ["fin"], ["soff"])
+        if t == 0:
+            ts(T.col[:, 5:6], T.col[:, 0:1], 2.0, None, A.mult, None, ["col0"], ["col5"])
         cp(at[:].indirect(T.soff[:]), T.ones[:, 0:96], ["soff", "ones"], [AT])
         cp(kt[:].indirect(T.soff[:]), T.m4[:], ["soff", "m4"], [KT])
         if t == 0:
-            ts(T.col[:, 2:3], T.col[:, 0:1], -0.75, qf, A.mult, A.add, ["col0", "qf"], ["col2"])
-            ts(T.col[:, 4:5], T.col[:, 0:1], -2.0, NONE, A.mult, A.add, ["col0"], ["col4"])
-            ts(T.col[:, 5:6], T.col[:, 0:1], 2.0, None, A.mult, None, ["col0"], ["col5"])
             ts(T.col[:, 3:4], T.col[:, 2:3], 192.0, None, A.add, None, ["col2"], ["col3"])
-            for b in range(4):
+            for b in range(2, 4):
                 quant(T.qe[:, 128 * b:128 * b + 128], T.se[:, 128 * b:128 * b + 128], T.eb[:, 3 - b:515 - b], ["eb"], ["qe%d" % b])
         if t == 1:
             quant(T.qv[:], T.sv[:], T.vt[:], ["vt"], ["qv"])
         arrival(t, "aw%d" % t, 1, [LW])
         arrival(t, "ac%d" % t, 2, LC[:1])
         arrival(t, "ad%d" % t, 1, LC[1:])
+        if t == 0:
+            dma("s", T.qw[:].bitcast(dt.uint8), T.wc[:], [WD], ["qw"], "ldw")
+            dma("s", T.sw[:], T.ws[:], [], ["sw"], "lds")
+            dma("s", T.vt[:], T.v[:], ["qw"], ["vt"], "ldv")
         act(T.pd0[:, 0:2 * C:2], at[:].indirect(lwd[:]), [AT, LW], ["pda"])
         ts(T.pd0[:, 1:2 * C:2], kt[:].indirect(lwd[:]), 384.0, 1.0 / 384.0, A.max, A.mult, [KT, LW], ["pdb"])
         act(T.key[:], kt[:].indirect(lwd[:]), [KT, LW], ["key"])
@@ -244,10 +219,9 @@ def rank_program(g, core, T, topo):
                 mm(4 * (1 - h) + b, HALF, T.qe[:, 128 * b:128 * b + 128], T.se[:, 128 * b:128 * b + 128],
                    lc[:, cols(h)], ls[:, cols(h)], LC[:h + 1] + ["qe%d" % b])
         scan(T.vb[:, 1:2 * C + 1], T.pd0[:], T.pd1[:], float(BASE + 124), A.mult, A.add, ["pda", "pdb", "pd1a", "pd1b"], ["vb"])
+        act(T.sg[:], T.vb[:, 0:2 * C:2], ["vb", "vb0"], ["sg"], ACT.Sign, bias=float(2 - BASE))
         for k in range(8):
             h, b = k // 4, k % 4
-            if k == 2:
-                act(T.sg[:], T.vb[:, 0:2 * C:2], ["vb", "vb0"], ["sg"], ACT.Sign, bias=float(2 - BASE))
             lo = 2 * C * b + C + HALF * h
             act(win[:, lo:lo + HALF], ps(4 * (1 - h) + b, HALF), [], ["ps%d" % (4 * (1 - h) + b), "d%d%d" % (b, h)], scale=64.0)
         for h in range(2):
@@ -265,7 +239,11 @@ def rank_program(g, core, T, topo):
         ts(T.si[:], T.hsel[:, 15:C:16], T.col[:, 5:6], None, A.add, None, ["hsel", "col5"], ["si"])
         tt(T.sm[:], T.sa[:], T.lw[:], A.min, ["sa", "lw"], ["sm"])
         ts(T.sb[:], T.si[:], 511, None, A.bitwise_and, None, ["si"], ["sb"])
+        if t == 0:
+            ts(win[:, 4 * C:5 * C], T.x0[:, 2:4 * C:4], 64.0, None, A.mult, None, xkeys(0) + xkeys(1), ["y20", "y21"])
         tt(T.ofp[:, 0:24], T.sm[:], T.sb[:], A.max, ["sm", "sb"], ["ofp"])
+        if t == 0:
+            ts(win[:, 6 * C:7 * C], T.x0[:, 3:4 * C:4], 64.0, None, A.mult, None, xkeys(0) + xkeys(1), ["y30", "y31"])
         cp(T.goff[:], T.ofp[:, 0:24], ["ofp"], ["goff"])
         for b in range(4):
             src = win[:, 2 * C * b:2 * C * b + 2 * C].indirect(T.goff[:])
@@ -275,13 +253,13 @@ def rank_program(g, core, T, topo):
             else:
                 act(T.gt[:, b:4 * C:4], src, need, ["g%d" % b], scale=0.015625)
         G = ["g%d" % b for b in range(4)]
+        ts(T.g64[:, 0:HALF], T.gt[:, 0:2 * C:4], 64.0, None, A.mult, None, ["g0"], ["h00"])
         for h in range(2):
             quant(T.qg[:, cols(h)], T.sgq[:, cols(h)], T.gt[:, 2 * C * h:2 * C * h + 2 * C], G, ["qg%d" % h])
         for h in range(2):
             for b in range(4):
                 mm(4 * h + b, HALF, T.qw[:, 128 * b:128 * b + 128], T.sw[:, 128 * b:128 * b + 128],
                    T.qg[:, cols(h)], T.sgq[:, cols(h)], ["qg%d" % h, "qw", "sw"])
-        ts(T.g64[:, 0:HALF], T.gt[:, 0:2 * C:4], 64.0, None, A.mult, None, ["g0"], ["h00"])
         for b in range(1, 4):
             act(T.g64[:, C * b:C * b + C], T.gt[:, b:4 * C:4], ["g%d" % b], ["h%d0" % b, "h%d1" % b], scale=64.0)
         act(T.g64[:, HALF:C], T.gt[:, 2 * C:4 * C:4], ["g0"], ["h01"], scale=64.0)

from concourse.mybir import dt, AluOpType, ActivationFunctionType

C, ROUNDS, STEP = 384, 3, [1, 2, 4]
F32, BF16, F16, I32, U16, Q4, U8 = "float32", "bfloat16", "float16", "int32", "uint16", "float8_e4m3fn_x4", "uint8"
HALF = C // 2
TAB = 640
SCRATCH = {"ps": ("psum", [128, 512 * 8], F32)}
for _d, _names in [
        (BF16, dict(x0=4 * C, ut=512, vt=512, ones=TAB, eb=516, selh=C, selc=C, key=C, sg=C, csel=C, gt=4 * C, g64=4 * C, xt=4 * C,
                    win0=8 * C, win1=8 * C, win2=8 * C, win3=8 * C)),
        (Q4, dict(qu=128, qu2=256, qv=128, qw=512, qe=512, qg=C, qx0=C, qx1=C, qx2=C, qx3=C, lc0=C, lc1=C, lc2=C)),
        (U8, dict(su=128, su2=256, sv=128, sw=512, se=512, sgq=C, sx0=C, sx1=C, sx2=C, sx3=C, ls0=C, ls1=C, ls2=C)),
        (I32, dict(ip=1, qi=1, iu=16, xi=C, yi=C, si=24, sb=24)),
        (U16, dict(uoff=16, qoff=24, soff=6, goff=24, lw0=24, lw1=24, lw2=24, wd0=24, wd1=24, wd2=24)),
        (F16, dict(c4=588, blk=98, ne=588, fin=588, hd0=C, hold=C, hsel=C)),
        (F32, dict(qf=1, col=6, j97=97, m4=96, d97=97, e0=16, e1=16, pat=16, selw=C, cd0=2 * C, pd1=2 * C, bits=2 * C, cod=776,
                   wsel=C, bsel=96, tgt=6, pd0=2 * C, vb=770, l0=24, lw=24, sa=24, sm=24, ofp=32, ht=32, ysb=C,
                   kt0=TAB, kt1=TAB, kt2=TAB, at0=TAB, at1=TAB, at2=TAB))]:
    for _n in _names:
        SCRATCH[_n] = ("sbuf", [128, _names[_n]], _d)

POOL = 110
SEMAPHORES = (["c%d" % i for i in range(POOL)] + ["ldx0", "ldx1", "ldu", "ldw", "lds", "ldv", "sts", "sta", "sent"]
              + ["%s%d" % (n, t) for n in ("ac", "ad", "aw") for t in range(ROUNDS)])

NONE = 512.0
BASE = 13400032
SHRINK = 0.75 - 2.0 ** -23
UNIT = 62.5
CUT = 360


def rank_program(g, core, T, topo):
    rank = T.rank_of(core)
    if rank is None:
        return
    A, ACT = AluOpType, ActivationFunctionType
    queue = {"v": g.vector, "a": g.scalar, "p": g.tensor, "g": g, "s": g.sync}
    ops = []

    def op(q, fn, r=(), w=(), sem=None, n=1):
        ops.append({"q": q, "fn": fn, "r": list(r), "w": list(w), "sem": sem, "n": n})

    def ts(out, in0, s1, s2, o0, o1, r, w):
        if o1 is None:
            op("v", lambda: g.vector.tensor_scalar(out, in0, s1, None, o0), r, w)
        else:
            op("v", lambda: g.vector.tensor_scalar(out, in0, s1, s2, o0, o1), r, w)

    def tt(out, in0, in1, o, r, w):
        op("v", lambda: g.vector.tensor_tensor(out, in0, in1, o), r, w)

    def cp(out, in_, r, w):
        op("v", lambda: g.vector.tensor_copy(out, in_), r, w)

    def scan(out, d0, d1, init, o0, o1, r, w):
        op("v", lambda: g.vector.tensor_tensor_scan(out, d0, d1, init, o0, o1), r, w)

    def fill(ap, c, w):
        op("v", lambda: g.vector.memset(ap, c), [], w)

    def quant(q, s, t, r, w):
        op("v", lambda: g.vector.quantize_mx(q, s, t), r, w)

    def act(out, in_, r, w, func=None, **kw):
        op("a", lambda: g.scalar.activation(out, in_, ACT.Copy if func is None else func, **kw), r, w)

    def afill(ap, n, c, w):
        act(ap, T.ones[:, 0:n], ["ones"], w, ACT.Identity, bias=c, scale=0.0)

    def mm(bank, n, ql, sl, qr, sr, r):
        op("p", lambda: g.tensor.matmul_mx(T.ps[:, 512 * bank:512 * bank + n], ql, sl, qr, sr, True, True), r, ["ps%d" % bank])

    def ps(bank, n):
        return T.ps[:, 512 * bank:512 * bank + n]

    def dma(q, out, in_, r, w, sem):
        op(q, lambda: queue[q].dma_start(out, in_), r, w, sem, 16)

    def iota(out, pat, base, mult, w, small):
        if small:
            op("g", lambda: g.iota(out, pat, base, mult, allow_small_or_imprecise_dtypes=True), [], w)
        else:
            op("g", lambda: g.iota(out, pat, base, mult), [], w)

    sent = [0]

    def send(t, out, in_, sem, r):
        peer = T.cores[rank ^ STEP[t]]
        rid, pid = topo.addr(peer)[0:2]
        sent[0] += len(topo.engines(core, peer))
        op("g", lambda: g.remote_dma(out, in_, T.sem[sem], T.sem.sent, pid, rid, topo.mask(core, peer)), r, [], "none")

    def arrival(t, sem, calls, w):
        peer = T.cores[rank ^ STEP[t]]
        op("x", None, [], w, sem, calls * len(topo.engines(peer, core)))

    def cols(h):
        return slice(HALF * h, HALF * h + HALF)

    def xkeys(h):
        return ["x%d%d" % (b, h) for b in range(4)]

    dma("a", T.ut[:], T.u[:], [], ["ut"], "ldu")
    for h in range(2):
        dma("s", T.x0[:, 2 * C * h:2 * C * h + 2 * C], T.x[:, 2 * C * h:2 * C * h + 2 * C], [], xkeys(h), "ldx%d" % h)

    fill(T.ones[:], 1.0, ["ones"])
    fill(T.cod[:, 2 * C:776], 628.0 / UNIT, ["codt"])
    fill(T.vb[:, 0:1], float(BASE + 124), ["vb0"])
    fill(T.ofp[:, 24:32], 0.0, ["ofpt"])
    iota(T.ip[:], [[0, 1]], 0, 1, ["ip"], False)
    iota(T.j97[:], [[1, 97]], 0, 0, ["j97"], True)
    iota(T.iu[:], [[1, 2], [16, 8]], 0, 0, ["iu"], False)
    op("g", lambda: g.affine_select(T.eb[:], T.ones[:, 0:516], [[1, 516]], A.is_equal, 0.0, -3, -4), ["ones"], ["eb"])
    iota(T.m4[:], [[4, 96]], 0, 0, ["m4"], True)
    afill(T.cd0[:, 0:2 * C:2], C, 0.05, ["cd0a"])
    afill(T.cd0[:, 1:2 * C:2], C, 4.0, ["cd0b"])
    afill(T.at0[:], TAB, SHRINK, ["at0"])
    ts(T.qi[:], T.ip[:], 15, None, A.bitwise_and, None, ["ip"], ["qi"])
    cp(T.qf[:], T.qi[:], ["qi"], ["qf"])
    ts(T.blk[:, 0:1], T.j97[:, 0:1], 0.0, None, A.mult, None, ["j97"], ["blk0"])
    qf = T.qf[:, 0:1]
    ts(T.d97[:], T.j97[:], qf, None, A.subtract, None, ["j97", "qf"], ["d97"])
    ts(T.qoff[:], T.j97[:, 0:24], 0.0, qf, A.mult, A.add, ["j97", "qf"], ["qoff"])
    ts(T.col[:, 0:1], qf, 15.0, 1024.0, A.is_lt, A.mult, ["qf"], ["col0"])
    ts(T.e0[:], T.d97[:, 0:16], 0.0, -4.0, A.is_equal, A.mult, ["d97"], ["e0"])
    ts(T.e1[:], T.d97[:, 0:16], 1.0, None, A.is_equal, None, ["d97"], ["e1"])
    cp(T.uoff[:], T.iu[:], ["iu"], ["uoff"])
    tt(T.pat[:], T.e0[:], T.e1[:], A.add, ["e0", "e1"], ["pat"])
    act(T.selw[:], T.pat[:].indirect(T.qoff[:]), ["pat", "qoff"], ["selw"], scale=1024.0)
    ts(T.col[:, 1:2], T.col[:, 0:1], UNIT, None, A.mult, None, ["col0"], ["col1"])
    for k in range(6):
        ts(T.c4[:, 98 * k + 1:98 * k + 97], T.d97[:, 1:97], 16.0 * k + 1, -1024.0, A.is_equal, A.mult, ["d97"], ["c4%d" % k])
    ts(T.c4[:, 0:588:98], T.j97[:, 0:6], 0.0, 2048.0, A.mult, A.add, ["j97"], ["c4h"])
    C4 = ["c4%d" % k for k in range(6)] + ["c4h", "c4t"]
    quant(T.qu[:], T.su[:], T.ut[:], ["ut"], ["qu"])
    quant(T.qe[:, 0:128], T.se[:, 0:128], T.eb[:, 3:515], ["eb"], ["qe0"])
    cp(T.qu2[:].bitcast(dt.uint32), T.qu[:].bitcast(dt.uint32).indirect(T.uoff[:]), ["qu", "uoff"], ["qu2"])
    act(T.su2[:], T.su[:].indirect(T.uoff[:]), ["qu", "uoff"], ["su2"])

    def quant_x(t, h):
        tile = T.x0 if t == 0 else T.xt
        quant(T["qx%d" % t][:, cols(h)], T["sx%d" % t][:, cols(h)], tile[:, 2 * C * h:2 * C * h + 2 * C], xkeys(h), ["qx%d%d" % (t, h)])

    quant_x(0, 0)
    quant(T.qe[:, 128:256], T.se[:, 128:256], T.eb[:, 2:514], ["eb"], ["qe1"])
    quant_x(0, 1)
    for t in range(ROUNDS):
        win, nxt, qx, sx = T["win%d" % t], T["win%d" % (t + 1)], T["qx%d" % t], T["sx%d" % t]
        lc, ls, lwd, wd, kt, at = T["lc%d" % t], T["ls%d" % t], T["lw%d" % t], T["wd%d" % t], T["kt%d" % t], T["at%d" % t]
        QX, KT, AT, LW, WD = ["qx%d0" % t, "qx%d1" % t], "kt%d" % t, "at%d" % t, "lw%d" % t, "wd%d" % t
        LC = ["lc%d0" % t, "lc%d1" % t]
        send(t, lc[:, cols(0)].bitcast(dt.uint8), qx[:, cols(0)].bitcast(dt.uint8), "ac%d" % t, QX[:1])
        for h in range(2):
            for s in range(2):
                mm(2 * h + s, HALF, T.qu2[:, 128 * s:128 * s + 128], T.su2[:, 128 * s:128 * s + 128],
                   qx[:, cols(h)], sx[:, cols(h)], [QX[h], "qu2", "su2"])
        for h in range(2):
            act(T.bits[:, C * h + 1:C * h + C:2], ps(2 * h + 1, HALF), [], ["ps%d" % (2 * h + 1), "bb%d" % h], ACT.Sign, bias=-2.0 ** -110)
        ts(T.bits[:, 0:C:2], ps(0, HALF), 0.0, 0.6584, A.is_gt, A.add, [], ["ps0", "ba0"])
        scan(T.cod[:, 0:CUT], T.cd0[:, 0:CUT], T.bits[:, 0:CUT], 2.042, A.mult, A.add, ["cd0a", "cd0b", "ba0", "bb0"], ["cod0"])
        ts(T.bits[:, C:2 * C:2], ps(2, HALF), 0.0, 0.6584, A.is_gt, A.add, [], ["ps2", "ba1"])
        scan(T.wsel[:, 0:176], T.selw[:, 0:176], T.cod[:, 7:359:2], 0.0, A.add, A.max, ["selw", "cod0"], ["wsel0"])
        scan(T.cod[:, CUT:2 * C], T.cd0[:, CUT:2 * C], T.bits[:, CUT:2 * C], T.cod[:, CUT - 1:CUT], A.mult, A.add,
             ["cod0", "ba0", "bb0", "ba1", "bb1"], ["cod1"])
        scan(T.wsel[:, 176:C], T.selw[:, 176:C], T.cod[:, 359:775:2], 0.0, A.add, A.max, ["selw", "cod0", "cod1", "codt"], ["wsel1"])
        ts(T.blk[:, 1:97], T.cod[:, 7:775:8], UNIT, 1024.0, A.mult, A.add, ["cod0", "cod1"], ["blk"])
        ts(wd[:], T.wsel[:, 15:C:16], UNIT, T.col[:, 1:2], A.mult, A.subtract, ["wsel0", "wsel1", "col1"], [WD])
        send(t, lwd[:], wd[:], "aw%d" % t, [WD])
        send(t, ls[:], sx[:], "ac%d" % t, QX)
        send(t, lc[:, cols(1)].bitcast(dt.uint8), qx[:, cols(1)].bitcast(dt.uint8), "ad%d" % t, QX[1:])
        if t > 0:
            afill(at[:], TAB, SHRINK, [AT])
        afill(kt[:], TAB, NONE, [KT])
        if t == 0:
            afill(T.pd1[:, 0:2 * C:2], C, 5.0, ["pd1a"])
            afill(T.pd1[:, 1:2 * C:2], C, -4.0, ["pd1b"])
            act(T.selh[:], T.selw[:], ["selw"], ["selh"], scale=-2.0)
            afill(T.pd1[:, 7:2 * C:8], C // 4, -8.0, ["pd1b"])
            act(T.selc[:], T.selw[:], ["selw"], ["selc"], scale=1.0 / 256)
            for b in range(2):
                act(win[:, 2 * C * b:2 * C * b + C], T.x0[:, b:4 * C:4], xkeys(0) + xkeys(1), ["y%d0" % b, "y%d1" % b], scale=64.0)
        scan(T.bsel[:], T.selw[:, 0:96], T.blk[:, 1:97], 0.0, A.add, A.max, ["selw", "blk"], ["bsel"])
        if t == 0:
            ts(T.c4[:, 97:588:98], T.m4[:, 0:24:4], qf, 1024.0, A.add, A.add, ["m4", "qf"], ["c4t"])
        ts(T.tgt[:], T.bsel[:, 15:96:16], T.col[:, 0:1], None, A.subtract, None, ["bsel", "col0"], ["tgt"])
        ts(T.ne[:, 97:588:98], T.bsel[:, 15:96:16], T.col[:, 0:1], 1024.0, A.subtract, A.subtract, ["bsel", "col0"], ["net"])
        for k in range(6):
            ts(T.ne[:, 98 * k:98 * k + 97], T.blk[:, 0:97], T.tgt[:, k:k + 1], 640.0, A.not_equal, A.mult, ["blk", "blk0", "tgt"], ["ne%d" % k])
        if t == 0:
            ts(T.col[:, 2:3], T.col[:, 0:1], -0.75, qf, A.mult, A.add, ["col0", "qf"], ["col2"])
        scan(T.fin[:], T.c4[:], T.ne[:], 0.0, A.add, A.min, C4 + ["net"] + ["ne%d" % k for k in range(6)], ["fin"])
        if t == 0:
            ts(T.col[:, 4:5], T.col[:, 0:1], -2.0, NONE, A.mult, A.add, ["col0"], ["col4"])
        cp(T.soff[:], T.fin[:, 97:588:98], ["fin"], ["soff"])
        if t == 0:
            ts(T.col[:, 5:6], T.col[:, 0:1], 2.0, None, A.mult, None, ["col0"], ["col5"])
        cp(at[:].indirect(T.soff[:]), T.ones[:, 0:96], ["soff", "ones"], [AT])
        cp(kt[:].indirect(T.soff[:]), T.m4[:], ["soff", "m4"], [KT])
        if t == 0:
            ts(T.col[:, 3:4], T.col[:, 2:3], 192.0, None, A.add, None, ["col2"], ["col3"])
            for b in range(2, 4):
                quant(T.qe[:, 128 * b:128 * b + 128], T.se[:, 128 * b:128 * b + 128], T.eb[:, 3 - b:515 - b], ["eb"], ["qe%d" % b])
        if t == 1:
            quant(T.qv[:], T.sv[:], T.vt[:], ["vt"], ["qv"])
        arrival(t, "aw%d" % t, 1, [LW])
        arrival(t, "ac%d" % t, 2, LC[:1])
        arrival(t, "ad%d" % t, 1, LC[1:])
        if t == 0:
            dma("s", T.qw[:].bitcast(dt.uint8), T.wc[:], [WD], ["qw"], "ldw")
            dma("s", T.sw[:], T.ws[:], [], ["sw"], "lds")
            dma("s", T.vt[:], T.v[:], ["qw"], ["vt"], "ldv")
        act(T.pd0[:, 0:2 * C:2], at[:].indirect(lwd[:]), [AT, LW], ["pda"])
        ts(T.pd0[:, 1:2 * C:2], kt[:].indirect(lwd[:]), 384.0, 1.0 / 384.0, A.max, A.mult, [KT, LW], ["pdb"])
        act(T.key[:], kt[:].indirect(lwd[:]), [KT, LW], ["key"])
        for h in range(2):
            for b in range(4):
                mm(4 * (1 - h) + b, HALF, T.qe[:, 128 * b:128 * b + 128], T.se[:, 128 * b:128 * b + 128],
                   lc[:, cols(h)], ls[:, cols(h)], LC[:h + 1] + ["qe%d" % b])
        scan(T.vb[:, 1:2 * C + 1], T.pd0[:], T.pd1[:], float(BASE + 124), A.mult, A.add, ["pda", "pdb", "pd1a", "pd1b"], ["vb"])
        act(T.sg[:], T.vb[:, 0:2 * C:2], ["vb", "vb0"], ["sg"], ACT.Sign, bias=float(2 - BASE))
        for k in range(8):
            h, b = k // 4, k % 4
            lo = 2 * C * b + C + HALF * h
            act(win[:, lo:lo + HALF], ps(4 * (1 - h) + b, HALF), [], ["ps%d" % (4 * (1 - h) + b), "d%d%d" % (b, h)], scale=64.0)
        for h in range(2):
            ts(T.xi[:, cols(h)], T.vb[:, C * h:C * h + C:2], float(BASE - 512), 8192.0, A.subtract, A.mult, ["vb", "vb0"], ["xi%d" % h])
        for h in range(2):
            ts(T.yi[:, cols(h)], T.xi[:, cols(h)], 3 << 13, None, A.bitwise_and, None, ["xi%d" % h], ["yi%d" % h])
        for h in range(2):
            ts(T.hd0[:, cols(h)], T.yi[:, cols(h)], 4096.0, 513.0, A.subtract, A.min, ["yi%d" % h], ["hd%d" % h])
        scan(T.csel[:], T.selc[:], T.sg[:], 0.0, A.add, A.max, ["selc", "sg"], ["csel"])
        scan(T.hold[:], T.hd0[:], T.key[:], 0.0, A.add, A.max, ["hd0", "hd1", "key"], ["hold"])
        ts(T.l0[:], T.csel[:, 15:C:16], 192.0, T.col[:, 3:4], A.mult, A.add, ["csel", "col3"], ["l0"])
        scan(T.hsel[:], T.selh[:], T.hold[:], 0.0, A.add, A.min, ["selh", "hold"], ["hsel"])
        tt(T.lw[:], T.l0[:], T.m4[:, 0:96:4], A.add, ["l0", "m4"], ["lw"])
        ts(T.sa[:], T.hsel[:, 15:C:16], T.col[:, 4:5], 4096.0, A.is_equal, A.mult, ["hsel", "col4"], ["sa"])
        ts(T.si[:], T.hsel[:, 15:C:16], T.col[:, 5:6], None, A.add, None, ["hsel", "col5"], ["si"])
        tt(T.sm[:], T.sa[:], T.lw[:], A.min, ["sa", "lw"], ["sm"])
        ts(T.sb[:], T.si[:], 511, None, A.bitwise_and, None, ["si"], ["sb"])
        if t == 0:
            ts(win[:, 4 * C:5 * C], T.x0[:, 2:4 * C:4], 64.0, None, A.mult, None, xkeys(0) + xkeys(1), ["y20", "y21"])
        tt(T.ofp[:, 0:24], T.sm[:], T.sb[:], A.max, ["sm", "sb"], ["ofp"])
        if t == 0:
            ts(win[:, 6 * C:7 * C], T.x0[:, 3:4 * C:4], 64.0, None, A.mult, None, xkeys(0) + xkeys(1), ["y30", "y31"])
        cp(T.goff[:], T.ofp[:, 0:24], ["ofp"], ["goff"])
        for b in range(4):
            src = win[:, 2 * C * b:2 * C * b + 2 * C].indirect(T.goff[:])
            need = ["y%d0" % b, "y%d1" % b, "d%d0" % b, "d%d1" % b, "goff"]
            if b < 2:
                ts(T.gt[:, b:4 * C:4], src, 0.015625, None, A.mult, None, need, ["g%d" % b])
            else:
                act(T.gt[:, b:4 * C:4], src, need, ["g%d" % b], scale=0.015625)
        G = ["g%d" % b for b in range(4)]
        ts(T.g64[:, 0:HALF], T.gt[:, 0:2 * C:4], 64.0, None, A.mult, None, ["g0"], ["h00"])
        for h in range(2):
            quant(T.qg[:, cols(h)], T.sgq[:, cols(h)], T.gt[:, 2 * C * h:2 * C * h + 2 * C], G, ["qg%d" % h])
        for h in range(2):
            for b in range(4):
                mm(4 * h + b, HALF, T.qw[:, 128 * b:128 * b + 128], T.sw[:, 128 * b:128 * b + 128],
                   T.qg[:, cols(h)], T.sgq[:, cols(h)], ["qg%d" % h, "qw", "sw"])
        for b in range(1, 4):
            act(T.g64[:, C * b:C * b + C], T.gt[:, b:4 * C:4], ["g%d" % b], ["h%d0" % b, "h%d1" % b], scale=64.0)
        act(T.g64[:, HALF:C], T.gt[:, 2 * C:4 * C:4], ["g0"], ["h01"], scale=64.0)
        if t == ROUNDS - 1:
            op("v", lambda: g.vector.transpose(T.ht[:], T.ofp[:]), ["ofp", "ofpt"], ["ht"])
            for k in range(8):
                dma("s", T.ot[k, :], T.ht[32 * (k // 2):32 * (k // 2) + 24, 16 * (k % 2):16 * (k % 2) + 16], ["ht"], [], "sts")
        for h in range(2):
            for b in range(4):
                lo = 2 * C * b + HALF * h
                tt(nxt[:, lo:lo + HALF], ps(4 * h + b, HALF), T.g64[:, C * b + HALF * h:C * b + HALF * h + HALF], A.add,
                   ["h%d%d" % (b, h)], ["ps%d" % (4 * h + b), "y%d%d" % (b, h)])
        for h, b in [(0, 0), (0, 1), (0, 2), (0, 3), (1, 0), (1, 1)]:
            lo = 2 * C * b + HALF * h
            act(T.xt[:, 2 * C * h + b:2 * C * h + 2 * C:4], nxt[:, lo:lo + HALF], ["y%d%d" % (b, h)], ["x%d%d" % (b, h)], scale=0.015625)
        quant_x(t + 1, 0)
        for b in range(2, 4):
            lo = 2 * C * b + HALF
            ts(T.xt[:, 2 * C + b:4 * C:4], nxt[:, lo:lo + HALF], 0.015625, None, A.mult, None, ["y%d1" % b], ["x%d1" % b])
        quant_x(t + 1, 1)

    qx, sx = T.qx3, T.sx3
    for h in range(2):
        mm(h, HALF, T.qv[:], T.sv[:], qx[:, cols(h)], sx[:, cols(h)], ["qx3%d" % h, "qv"])
        dma("s", T.oc[:, 2 * C * h:2 * C * h + 2 * C], qx[:, cols(h)].bitcast(dt.uint8), ["qx3%d" % h], [], "sts")
    act(T.ysb[:, cols(0)], ps(0, HALF), [], ["ps0", "ys0"])
    cp(T.ysb[:, cols(1)], ps(1, HALF), [], ["ps1", "ys1"])
    dma("a", T.y[:, cols(0)], T.ysb[:, cols(0)], ["ys0"], [], "sta")
    for k in range(4):
        dma("a" if k % 2 else "s", T.osc[4 * k:4 * k + 4, :], sx[32 * k:32 * k + 4, :], ["qx30", "qx31"], [], "sta" if k % 2 else "sts")
    dma("s", T.y[:, cols(1)], T.ysb[:, cols(1)], ["ys1"], [], "sts")

    writer, readers, known = {}, {}, {q: 0 for q in "vapgsx"}
    for i, o in enumerate(ops):
        deps = set()
        for k in o["r"] + o["w"]:
            if k in writer:
                deps.add(writer[k])
        for k in o["w"]:
            deps.update(readers.get(k, []))
        o["waits"] = []
        for d in sorted(deps, reverse=True):
            if not known[o["q"]] >> d & 1:
                o["waits"].append(d)
                known[o["q"]] |= ops[d]["known"] | 1 << d
                ops[d]["waited"] = True
        o["known"] = known[o["q"]]
        for k in o["r"]:
            readers.setdefault(k, []).append(i)
        for k in o["w"]:
            writer[k] = i
            readers[k] = []
    last_on, count, total = [], [], {}
    for i, o in enumerate(ops):
        if o["sem"] is not None:
            total[o["sem"]] = total.get(o["sem"], 0) + o["n"]
            o["val"] = total[o["sem"]]
        elif o.get("waited"):
            free = [s for s in range(len(last_on)) if o["known"] >> last_on[s] & 1]
            if free:
                s = free[0]
            else:
                s = len(last_on)
                last_on.append(i)
                count.append(0)
            last_on[s] = i
            count[s] += 1
            o["sem"], o["val"] = "c%d" % s, count[s]
    for o in ops:
        if o["q"] == "x":
            continue
        for d in o["waits"]:
            queue[o["q"]].wait_ge(T.sem[ops[d]["sem"]], ops[d]["val"])
        ins = o["fn"]()
        if o["sem"] is not None and o["sem"] != "none":
            ins.then_inc(T.sem[o["sem"]], o["n"])
    g.sync.wait_ge(T.sem.sts, total["sts"])
    g.scalar.wait_ge(T.sem.sta, total["sta"])
    g.wait_ge(T.sem.sent, sent[0])
